import numpy as np, ml_dtypes
CORES = [31,71,111]
N = 3
import mx_ref
NC, G, D = 256, 4, 32
C = np.float32(0.043)
BF = ml_dtypes.bfloat16
def cut(t, i, w=512):
    return t[:, w * i:w * i + w]
def tile(rs):
    return np.stack(rs, axis=2).reshape(128, -1).astype(BF)
def layer(w, X):
    out = []
    for i in range(G):
        for t in range(len(X)):
            p = mx_ref.matmul(mx_ref.quantize(cut(w, len(X) * i + t)), X[t])
            z = p if t == 0 else z + p
        out.append(z)
    return out
def act(Z):
    return [np.maximum(z, 0) * C for z in Z]
def setup_inputs(rng):
    def f(*shape):
        return mx_ref.flush((rng.standard_normal(shape, dtype=np.float32) * np.exp2(rng.integers(-2, 3, shape[:-1] + (1,)))).astype(BF))
    return {"x": f(N, 128, 4 * NC), "w1": f(N, 128, G * 512), "wt": f(N, 128, 3 * 512)}
def setup_inputs_blocks(rng):
    d = setup_inputs(rng)
    for k in ("x", "wt", "w1"): d[k] = mx_ref.spread(d[k], rng, 2)
    return d
def setup_inputs_wide(rng):
    d = setup_inputs(rng)
    for k in ("wt",): d[k] = mx_ref.flush((d[k].astype(np.float32) * np.exp2(rng.integers(-6, 7, (N, 1, 1))).astype(np.float32)).astype(BF))
    return d
def setup_inputs_zeros(rng):
    d = setup_inputs(rng); v = d["x"].reshape(N, 128, -1, 4).copy()
    v[np.broadcast_to((rng.random((N, 1, v.shape[2], 1)) < 0.33), v.shape)] = 0
    d["x"] = v.reshape(d["x"].shape)
    return d
def reference(x, w1, wt):
    h = [tile(act(layer(w1[j], [mx_ref.quantize(x[j])]))) for j in range(N)]
    y = np.zeros((N, 128, NC), np.float32)
    for r in range(N):
        e = np.concatenate([h[(r - 1) % N][:, 4 * (NC - D):], h[r], h[(r + 1) % N][:, :4 * D]], axis=1)
        for t in range(3):
            p = mx_ref.matmul(mx_ref.quantize(cut(wt[r], t)), mx_ref.quantize(e[:, 4 * D * t:4 * D * t + 4 * NC]))
            y[r] = p if t == 0 else y[r] + p
    return {"y": y}

@@ -1,0 +1,155 @@
+from concourse.bass import DstId, RemoteDMATransfer
+from concourse.mybir import dt, AluOpType, ActivationFunctionType
+
+NC, D, H = 256, 32, 128
+G, NT = 4, 3
+C = 0.043
+P0 = H
+
+SCRATCH = {
+    "xb": ("sbuf", [128, 4 * NC], "bfloat16"),
+    "w1b": ("sbuf", [128, G * 512], "bfloat16"),
+    "wtb": ("sbuf", [128, NT * 512], "bfloat16"),
+    "xq": ("sbuf", [128, NC], "float8_e4m3fn_x4"),
+    "xs": ("sbuf", [128, NC], "uint8"),
+    "w1q": ("sbuf", [128, G * 128], "float8_e4m3fn_x4"),
+    "w1s": ("sbuf", [128, G * 128], "uint8"),
+    "wtq": ("sbuf", [128, NT * 128], "float8_e4m3fn_x4"),
+    "wts": ("sbuf", [128, NT * 128], "uint8"),
+    "h": ("sbuf", [128, 4 * NC], "bfloat16"),
+    "E": ("sbuf", [128, NC + 2 * D], "float8_e4m3fn_x4"),
+    "P": ("sbuf", [128, NC + 2 * H], "uint8"),
+    "za": ("psum", [128, 512 * G], "float32"),
+    "zb": ("psum", [128, 512 * G], "float32"),
+    "yo": ("sbuf", [128, NC], "float32"),
+}
+SEMAPHORES = (["lx0", "lx1", "lw0", "lw1", "lt", "qx0", "qx1", "qt", "qh0", "qh1", "av0", "av1", "as0", "as1",
+               "arrL", "arrR", "sent", "y0", "y1", "c0", "c1", "st0", "st1"]
+              + ["qw%d" % i for i in range(G)] + ["z%d%d" % (k, i) for k in range(2) for i in range(G)])
+
+
+def rank_program(g, core, T, topo):
+    rank = T.rank_of(core)
+    if rank is None:
+        return
+    n = len(T.cores)
+    left, right = T.cores[(rank - 1) % n], T.cores[(rank + 1) % n]
+    s = T.sem
+    te, ve, sc, sy = g.tensor, g.vector, g.scalar, g.sync
+    Z = [T.za, T.zb]
+
+    last = (G - 1) * 512
+    sy.dma_start(T.w1b[:, 0:last], T.w1[:, 0:last]).then_inc(s.lw0, 16)
+    sc.dma_start(T.xb[:, 0:4 * H], T.x[:, 0:4 * H]).then_inc(s.lx0, 16)
+    sy.dma_start(T.w1b[:, last:], T.w1[:, last:]).then_inc(s.lw1, 16)
+    sy.dma_start(T.xb[:, 4 * H:], T.x[:, 4 * H:]).then_inc(s.lx1, 16)
+    sy.wait_ge(s.lx0, 16)
+    sy.dma_start(T.wtb[:], T.wt[:]).then_inc(s.lt, 16)
+
+    def q_w1(i):
+        ve.quantize_mx(T.w1q[:, 128 * i:128 * i + 128], T.w1s[:, 128 * i:128 * i + 128],
+                       T.w1b[:, 512 * i:512 * i + 512]).then_inc(s["qw%d" % i], 1)
+
+    def q_x(k):
+        ve.quantize_mx(T.xq[:, H * k:H * k + H], T.xs[:, H * k:H * k + H],
+                       T.xb[:, 4 * H * k:4 * H * k + 4 * H]).then_inc(s["qx%d" % k], 1)
+
+    def q_h(k):
+        ve.quantize_mx(T.E[:, D + H * k:D + H * k + H], T.P[:, P0 + H * k:P0 + H * k + H],
+                       T.h[:, 4 * H * k:4 * H * k + 4 * H]).then_inc(s["qh%d" % k], 1)
+
+    def h_cols(k, b):
+        return T.h[:, 4 * H * k + b:4 * H * k + 4 * H:G]
+
+    def act_v(k, b):
+        ve.wait_ge(s["z%d%d" % (k, b)], 1)
+        ve.tensor_scalar(h_cols(k, b), Z[k][:, 512 * b:512 * b + H], 0.0, C, AluOpType.max,
+                         AluOpType.mult).then_inc(s["av%d" % k], 1)
+
+    def act_s(k, b):
+        sc.wait_ge(s["z%d%d" % (k, b)], 1)
+        sc.activation(h_cols(k, b), Z[k][:, 512 * b:512 * b + H], ActivationFunctionType.Relu,
+                      scale=C).then_inc(s["as%d" % k], 1)
+
+    ve.wait_ge(s.lx0, 16)
+    q_x(0)
+    ve.wait_ge(s.lw0, 16)
+    for i in range(G - 1):
+        q_w1(i)
+    ve.wait_ge(s.lw1, 16)
+    q_w1(G - 1)
+    act_v(0, 3)
+    ve.wait_ge(s.av0, 1)
+    ve.wait_ge(s.as0, 3)
+    q_h(0)
+    ve.wait_ge(s.lx1, 16)
+    q_x(1)
+    act_v(1, 1)
+    act_v(1, 3)
+    ve.wait_ge(s.av1, 2)
+    ve.wait_ge(s.as1, 2)
+    q_h(1)
+    ve.wait_ge(s.lt, 16)
+    ve.quantize_mx(T.wtq[:], T.wts[:], T.wtb[:]).then_inc(s.qt, 1)
+    ve.wait_ge(s.y0, 1)
+    ve.tensor_copy(T.yo[:, 0:H], T.za[:, 0:H]).then_inc(s.c0, 1)
+
+    for b in (0, 1, 2):
+        act_s(0, b)
+    for b in (0, 2):
+        act_s(1, b)
+    sc.wait_ge(s.y1, 1)
+    sc.activation(T.yo[:, H:NC], T.za[:, 512:512 + H], ActivationFunctionType.Copy).then_inc(s.c1, 1)
+    sc.wait_ge(s.c1, 1)
+    sc.dma_start(T.y[:, H:NC], T.yo[:, H:NC]).then_inc(s.st1, 16)
+    sc.wait_ge(s.st1, 16)
+
+    for k in range(2):
+        te.wait_ge(s["qx%d" % k], 1)
+        for b in range(G):
+            if k == 0:
+                te.wait_ge(s["qw%d" % b], 1)
+            te.matmul_mx(Z[k][:, 512 * b:512 * b + H], T.w1q[:, 128 * b:128 * b + 128], T.w1s[:, 128 * b:128 * b + 128],
+                         T.xq[:, H * k:H * k + H], T.xs[:, H * k:H * k + H], True, True).then_inc(s["z%d%d" % (k, b)], 1)
+
+    def tap(k, t, start, stop):
+        e = D * t + H * k
+        p = P0 - D + e
+        return te.matmul_mx(T.za[:, 512 * k:512 * k + H], T.wtq[:, 128 * t:128 * t + 128], T.wts[:, 128 * t:128 * t + 128],
+                            T.E[:, e:e + H], T.P[:, p:p + H], start, stop)
+
+    te.wait_ge(s.qh0, 1)
+    te.wait_ge(s.qh1, 1)
+    te.wait_ge(s.qt, 1)
+    tap(0, 1, True, False)
+    tap(1, 1, True, False)
+    tap(0, 2, False, False)
+    tap(1, 0, False, False)
+    te.wait_ge(s.arrR, 4)
+    tap(1, 2, False, True).then_inc(s.y1, 1)
+    te.wait_ge(s.arrL, 4)
+    tap(0, 0, False, True).then_inc(s.y0, 1)
+
+    def send(dst, part, e_src, e_dst, p_src, p_dst, sem):
+        m = topo.mask(core, dst)
+        eng = [1 << i for i in range(m.bit_length()) if m >> i & 1]
+        q = len(eng) // 4
+        mk = [sum(eng[q * (2 * part + j):q * (2 * part + j) + q]) for j in range(2)]
+        rid, pid = topo.addr(dst)[:2]
+        to = [DstId(rid=rid, pnc=pid)]
+        g.remote_dma_fused([
+            RemoteDMATransfer(dst_ids=to, dma_engine_mask=mk[0], remote_sem=sem,
+                              src=T.E[:, e_src:e_src + D].bitcast(dt.uint8), dst=T.E[:, e_dst:e_dst + D].bitcast(dt.uint8)),
+            RemoteDMATransfer(dst_ids=to, dma_engine_mask=mk[1], remote_sem=sem,
+                              src=T.P[:, p_src:p_src + H], dst=T.P[:, p_dst:p_dst + H]),
+        ], local_sem=s.sent)
+
+    g.wait_ge(s.qh0, 1)
+    send(left, 0, D, D + NC, P0, P0 + NC, s.arrR)
+    g.wait_ge(s.qh1, 1)
+    send(right, 1, NC, 0, P0 + H, 0, s.arrL)
+    g.wait_ge(s.sent, 8)
+
+    sy.wait_ge(s.c0, 1)
+    sy.dma_start(T.y[:, 0:H], T.yo[:, 0:H]).then_inc(s.st0, 16)
+    sy.wait_ge(s.st0, 16)

@@ -5,6 +5,7 @@ NC, D, H = 256, 32, 128
 G, NT = 4, 3
 C = 0.043
 P0 = H
+PIECES = ((0, 2), (2, 3), (3, 4))
 
 SCRATCH = {
     "xb": ("sbuf", [128, 4 * NC], "bfloat16"),
@@ -23,8 +24,9 @@ SCRATCH = {
     "zb": ("psum", [128, 512 * G], "float32"),
     "yo": ("sbuf", [128, NC], "float32"),
 }
-SEMAPHORES = (["lx0", "lx1", "lw0", "lw1", "lt", "qx0", "qx1", "qt", "qh0", "qh1", "av0", "av1", "as0", "as1",
+SEMAPHORES = (["lx0", "lx1", "lt", "qx0", "qx1", "qt", "qh0", "qh1", "av1", "as0", "as1",
                "arrL", "arrR", "sent", "y0", "y1", "c0", "c1", "st0", "st1"]
+              + ["lw%d" % i for i in range(len(PIECES))]
               + ["qw%d" % i for i in range(G)] + ["z%d%d" % (k, i) for k in range(2) for i in range(G)])
 
 
@@ -38,10 +40,13 @@ def rank_program(g, core, T, topo):
     te, ve, sc, sy = g.tensor, g.vector, g.scalar, g.sync
     Z = [T.za, T.zb]
 
-    last = (G - 1) * 512
-    sy.dma_start(T.w1b[:, 0:last], T.w1[:, 0:last]).then_inc(s.lw0, 16)
-    sc.dma_start(T.xb[:, 0:4 * H], T.x[:, 0:4 * H]).then_inc(s.lx0, 16)
-    sy.dma_start(T.w1b[:, last:], T.w1[:, last:]).then_inc(s.lw1, 16)
+    def engines(src, dst):
+        m = topo.mask(src, dst)
+        return [1 << i for i in range(m.bit_length()) if m >> i & 1]
+
+    sy.dma_start(T.xb[:, 0:4 * H], T.x[:, 0:4 * H]).then_inc(s.lx0, 16)
+    for k, (a, b) in enumerate(PIECES):
+        sy.dma_start(T.w1b[:, 512 * a:512 * b], T.w1[:, 512 * a:512 * b]).then_inc(s["lw%d" % k], 16)
     sy.dma_start(T.xb[:, 4 * H:], T.x[:, 4 * H:]).then_inc(s.lx1, 16)
     sy.wait_ge(s.lx0, 16)
     sy.dma_start(T.wtb[:], T.wt[:]).then_inc(s.lt, 16)
@@ -73,17 +78,14 @@ def rank_program(g, core, T, topo):
 
     ve.wait_ge(s.lx0, 16)
     q_x(0)
-    ve.wait_ge(s.lw0, 16)
-    for i in range(G - 1):
-        q_w1(i)
-    ve.wait_ge(s.lw1, 16)
-    q_w1(G - 1)
-    act_v(0, 3)
-    ve.wait_ge(s.av0, 1)
-    ve.wait_ge(s.as0, 3)
-    q_h(0)
+    for k, (a, b) in enumerate(PIECES):
+        ve.wait_ge(s["lw%d" % k], 16)
+        for i in range(a, b):
+            q_w1(i)
     ve.wait_ge(s.lx1, 16)
     q_x(1)
+    ve.wait_ge(s.as0, G)
+    q_h(0)
     act_v(1, 1)
     act_v(1, 3)
     ve.wait_ge(s.av1, 2)
@@ -94,7 +96,7 @@ def rank_program(g, core, T, topo):
     ve.wait_ge(s.y0, 1)
     ve.tensor_copy(T.yo[:, 0:H], T.za[:, 0:H]).then_inc(s.c0, 1)
 
-    for b in (0, 1, 2):
+    for b in range(G):
         act_s(0, b)
     for b in (0, 2):
         act_s(1, b)
@@ -125,30 +127,29 @@ def rank_program(g, core, T, topo):
     tap(1, 1, True, False)
     tap(0, 2, False, False)
     tap(1, 0, False, False)
-    te.wait_ge(s.arrR, 4)
+    te.wait_ge(s.arrR, len(engines(right, core)))
     tap(1, 2, False, True).then_inc(s.y1, 1)
-    te.wait_ge(s.arrL, 4)
+    te.wait_ge(s.arrL, len(engines(left, core)))
     tap(0, 0, False, True).then_inc(s.y0, 1)
 
-    def send(dst, part, e_src, e_dst, p_src, p_dst, sem):
-        m = topo.mask(core, dst)
-        eng = [1 << i for i in range(m.bit_length()) if m >> i & 1]
-        q = len(eng) // 4
-        mk = [sum(eng[q * (2 * part + j):q * (2 * part + j) + q]) for j in range(2)]
+    def send(dst, e_src, e_dst, p_src, p_dst, sem):
+        eng = engines(core, dst)
+        q = len(eng) // 2
         rid, pid = topo.addr(dst)[:2]
         to = [DstId(rid=rid, pnc=pid)]
         g.remote_dma_fused([
-            RemoteDMATransfer(dst_ids=to, dma_engine_mask=mk[0], remote_sem=sem,
+            RemoteDMATransfer(dst_ids=to, dma_engine_mask=sum(eng[:q]), remote_sem=sem,
                               src=T.E[:, e_src:e_src + D].bitcast(dt.uint8), dst=T.E[:, e_dst:e_dst + D].bitcast(dt.uint8)),
-            RemoteDMATransfer(dst_ids=to, dma_engine_mask=mk[1], remote_sem=sem,
+            RemoteDMATransfer(dst_ids=to, dma_engine_mask=sum(eng[q:]), remote_sem=sem,
                               src=T.P[:, p_src:p_src + H], dst=T.P[:, p_dst:p_dst + H]),
         ], local_sem=s.sent)
+        return len(eng)
 
     g.wait_ge(s.qh0, 1)
-    send(left, 0, D, D + NC, P0, P0 + NC, s.arrR)
+    a = send(left, D, D + NC, P0, P0 + NC, s.arrR)
     g.wait_ge(s.qh1, 1)
-    send(right, 1, NC, 0, P0 + H, 0, s.arrL)
-    g.wait_ge(s.sent, 8)
+    b = send(right, NC, 0, P0 + H, 0, s.arrL)
+    g.wait_ge(s.sent, a + b)
 
     sy.wait_ge(s.c0, 1)
     sy.dma_start(T.y[:, 0:H], T.yo[:, 0:H]).then_inc(s.st0, 16)

from concourse.bass import DstId, RemoteDMATransfer
from concourse.mybir import dt, AluOpType, ActivationFunctionType

NC, D, H = 256, 32, 128
G, NT = 4, 3
C = 0.043
P0 = H
PIECES = ((0, 2), (2, 3), (3, 4))

SCRATCH = {
    "xb": ("sbuf", [128, 4 * NC], "bfloat16"),
    "w1b": ("sbuf", [128, G * 512], "bfloat16"),
    "wtb": ("sbuf", [128, NT * 512], "bfloat16"),
    "xq": ("sbuf", [128, NC], "float8_e4m3fn_x4"),
    "xs": ("sbuf", [128, NC], "uint8"),
    "w1q": ("sbuf", [128, G * 128], "float8_e4m3fn_x4"),
    "w1s": ("sbuf", [128, G * 128], "uint8"),
    "wtq": ("sbuf", [128, NT * 128], "float8_e4m3fn_x4"),
    "wts": ("sbuf", [128, NT * 128], "uint8"),
    "h": ("sbuf", [128, 4 * NC], "bfloat16"),
    "E": ("sbuf", [128, NC + 2 * D], "float8_e4m3fn_x4"),
    "P": ("sbuf", [128, NC + 2 * H], "uint8"),
    "za": ("psum", [128, 512 * G], "float32"),
    "zb": ("psum", [128, 512 * G], "float32"),
    "yo": ("sbuf", [128, NC], "float32"),
}
SEMAPHORES = (["lx0", "lx1", "lt", "qx0", "qx1", "qt", "qh0", "qh1", "av1", "as0", "as1",
               "arrL", "arrR", "sent", "y0", "y1", "c0", "c1", "st0", "st1"]
              + ["lw%d" % i for i in range(len(PIECES))]
              + ["qw%d" % i for i in range(G)] + ["z%d%d" % (k, i) for k in range(2) for i in range(G)])


def rank_program(g, core, T, topo):
    rank = T.rank_of(core)
    if rank is None:
        return
    n = len(T.cores)
    left, right = T.cores[(rank - 1) % n], T.cores[(rank + 1) % n]
    s = T.sem
    te, ve, sc, sy = g.tensor, g.vector, g.scalar, g.sync
    Z = [T.za, T.zb]

    def engines(src, dst):
        m = topo.mask(src, dst)
        return [1 << i for i in range(m.bit_length()) if m >> i & 1]

    sy.dma_start(T.xb[:, 0:4 * H], T.x[:, 0:4 * H]).then_inc(s.lx0, 16)
    for k, (a, b) in enumerate(PIECES):
        sy.dma_start(T.w1b[:, 512 * a:512 * b], T.w1[:, 512 * a:512 * b]).then_inc(s["lw%d" % k], 16)
    sy.dma_start(T.xb[:, 4 * H:], T.x[:, 4 * H:]).then_inc(s.lx1, 16)
    sy.wait_ge(s.lx0, 16)
    sy.dma_start(T.wtb[:], T.wt[:]).then_inc(s.lt, 16)

    def q_w1(i):
        ve.quantize_mx(T.w1q[:, 128 * i:128 * i + 128], T.w1s[:, 128 * i:128 * i + 128],
                       T.w1b[:, 512 * i:512 * i + 512]).then_inc(s["qw%d" % i], 1)

    def q_x(k):
        ve.quantize_mx(T.xq[:, H * k:H * k + H], T.xs[:, H * k:H * k + H],
                       T.xb[:, 4 * H * k:4 * H * k + 4 * H]).then_inc(s["qx%d" % k], 1)

    def q_h(k):
        ve.quantize_mx(T.E[:, D + H * k:D + H * k + H], T.P[:, P0 + H * k:P0 + H * k + H],
                       T.h[:, 4 * H * k:4 * H * k + 4 * H]).then_inc(s["qh%d" % k], 1)

    def h_cols(k, b):
        return T.h[:, 4 * H * k + b:4 * H * k + 4 * H:G]

    def act_v(k, b):
        ve.wait_ge(s["z%d%d" % (k, b)], 1)
        ve.tensor_scalar(h_cols(k, b), Z[k][:, 512 * b:512 * b + H], 0.0, C, AluOpType.max,
                         AluOpType.mult).then_inc(s["av%d" % k], 1)

    def act_s(k, b):
        sc.wait_ge(s["z%d%d" % (k, b)], 1)
        sc.activation(h_cols(k, b), Z[k][:, 512 * b:512 * b + H], ActivationFunctionType.Relu,
                      scale=C).then_inc(s["as%d" % k], 1)

    ve.wait_ge(s.lx0, 16)
    q_x(0)
    for k, (a, b) in enumerate(PIECES):
        ve.wait_ge(s["lw%d" % k], 16)
        for i in range(a, b):
            q_w1(i)
    ve.wait_ge(s.lx1, 16)
    q_x(1)
    ve.wait_ge(s.as0, G)
    q_h(0)
    act_v(1, 1)
    act_v(1, 3)
    ve.wait_ge(s.av1, 2)
    ve.wait_ge(s.as1, 2)
    q_h(1)
    ve.wait_ge(s.lt, 16)
    ve.quantize_mx(T.wtq[:], T.wts[:], T.wtb[:]).then_inc(s.qt, 1)
    ve.wait_ge(s.y0, 1)
    ve.tensor_copy(T.yo[:, 0:H], T.za[:, 0:H]).then_inc(s.c0, 1)

    for b in range(G):
        act_s(0, b)
    for b in (0, 2):
        act_s(1, b)
    sc.wait_ge(s.y1, 1)
    sc.activation(T.yo[:, H:NC], T.za[:, 512:512 + H], ActivationFunctionType.Copy).then_inc(s.c1, 1)
    sc.wait_ge(s.c1, 1)
    sc.dma_start(T.y[:, H:NC], T.yo[:, H:NC]).then_inc(s.st1, 16)
    sc.wait_ge(s.st1, 16)

    for k in range(2):
        te.wait_ge(s["qx%d" % k], 1)
        for b in range(G):
            if k == 0:
                te.wait_ge(s["qw%d" % b], 1)
            te.matmul_mx(Z[k][:, 512 * b:512 * b + H], T.w1q[:, 128 * b:128 * b + 128], T.w1s[:, 128 * b:128 * b + 128],
                         T.xq[:, H * k:H * k + H], T.xs[:, H * k:H * k + H], True, True).then_inc(s["z%d%d" % (k, b)], 1)

    def tap(k, t, start, stop):
        e = D * t + H * k
        p = P0 - D + e
        return te.matmul_mx(T.za[:, 512 * k:512 * k + H], T.wtq[:, 128 * t:128 * t + 128], T.wts[:, 128 * t:128 * t + 128],
                            T.E[:, e:e + H], T.P[:, p:p + H], start, stop)

    te.wait_ge(s.qh0, 1)
    te.wait_ge(s.qh1, 1)
    te.wait_ge(s.qt, 1)
    tap(0, 1, True, False)
    tap(1, 1, True, False)
    tap(0, 2, False, False)
    tap(1, 0, False, False)
    te.wait_ge(s.arrR, len(engines(right, core)))
    tap(1, 2, False, True).then_inc(s.y1, 1)
    te.wait_ge(s.arrL, len(engines(left, core)))
    tap(0, 0, False, True).then_inc(s.y0, 1)

    def send(dst, e_src, e_dst, p_src, p_dst, sem):
        eng = engines(core, dst)
        q = len(eng) // 2
        rid, pid = topo.addr(dst)[:2]
        to = [DstId(rid=rid, pnc=pid)]
        g.remote_dma_fused([
            RemoteDMATransfer(dst_ids=to, dma_engine_mask=sum(eng[:q]), remote_sem=sem,
                              src=T.E[:, e_src:e_src + D].bitcast(dt.uint8), dst=T.E[:, e_dst:e_dst + D].bitcast(dt.uint8)),
            RemoteDMATransfer(dst_ids=to, dma_engine_mask=sum(eng[q:]), remote_sem=sem,
                              src=T.P[:, p_src:p_src + H], dst=T.P[:, p_dst:p_dst + H]),
        ], local_sem=s.sent)
        return len(eng)

    g.wait_ge(s.qh0, 1)
    a = send(left, D, D + NC, P0, P0 + NC, s.arrR)
    g.wait_ge(s.qh1, 1)
    b = send(right, NC, 0, P0 + H, 0, s.arrL)
    g.wait_ge(s.sent, a + b)

    sy.wait_ge(s.c0, 1)
    sy.dma_start(T.y[:, 0:H], T.yo[:, 0:H]).then_inc(s.st0, 16)
    sy.wait_ge(s.st0, 16)
